import numpy as np
import ml_dtypes


def mxq(x, axis, fmt="e4m3"):
    dtype, down = {"e4m3": (ml_dtypes.float8_e4m3fn, 7), "e5m2": (ml_dtypes.float8_e5m2, 14)}[fmt]
    v = np.moveaxis(np.asarray(x, np.float32).astype(ml_dtypes.bfloat16).astype(np.float64), axis, -1)
    blocks = v.reshape(v.shape[:-1] + (-1, 32))
    amax = np.abs(blocks).max(-1, keepdims=True)
    byte = np.maximum(np.where(amax > 0, np.frexp(amax)[1] - 1 + 127, 0) - down, 1)
    scale = np.exp2(byte - 127.0)
    codes = (blocks / scale).astype(np.float32).astype(dtype).astype(np.float64)
    return np.moveaxis((codes * scale).reshape(v.shape), -1, axis)


WIDE = False


def mx_kscale(k):
    if not WIDE:
        return np.ones(k)
    levels = np.array([24, -24, 12, -12, 0])
    if k % 512:
        return np.exp2(np.random.permutation(np.resize(levels, k // 32))).repeat(32)
    a = np.empty((k // 512, 16))
    for p in range(k // 512):
        a[p, :8] = np.random.permutation(np.resize(levels, 8))
        for g in range(8):
            far = levels[np.abs(levels - a[p, g]) >= 10]
            a[p, g + 8] = far[np.random.randint(len(far))]
    return np.exp2(a.ravel()).repeat(32)


def f64(x):
    return np.asarray(x).astype(np.float64)


def striped(idx):
    return np.tile(idx.reshape(-1, 16).T, (8, 1)).astype(np.uint16)


def unstriped(offs):
    return offs[:16].T.reshape(-1).astype(np.int64)


E2M1 = np.array([0.0, 0.5, 1.0, 1.5, 2.0, 3.0, 4.0, 6.0, -0.0, -0.5, -1.0, -1.5, -2.0, -3.0, -4.0, -6.0])


def pack_weight(w, fmt):
    k, n = w.shape
    w = f64(np.asarray(w, np.float32).astype(ml_dtypes.bfloat16)).reshape(k // 32, 32, n)
    amax = np.abs(w).max(1)
    if fmt == "e4m3":
        byte = np.frexp(amax)[1] - 1 + 127 - 7
    else:
        mant, ex = np.frexp(amax / 6.0)
        byte = np.where(mant > 0.5, ex, ex - 1) + 127
    byte = np.clip(np.where(amax > 0, byte, 1), 1, 254)
    scaled = (w * np.exp2(127.0 - byte)[:, None, :]).reshape(k, n).astype(np.float32)
    by_word = np.ascontiguousarray(scaled.reshape(k // 512, 128, 4, n).transpose(0, 1, 3, 2))
    if fmt == "e4m3":
        words = by_word.astype(ml_dtypes.float8_e4m3fn).view(np.uint8)
    else:
        c = by_word.astype(ml_dtypes.float4_e2m1fn).view(np.uint8) & 0xF
        words = (c[..., 0::2] | (c[..., 1::2] << 4)).reshape(k // 512, 128, 2 * n)
    return np.ascontiguousarray(words), np.ascontiguousarray(byte.astype(np.uint8).reshape(k // 512, 16, n))


def unpack_weight(words, scales, fmt):
    g, _, n = scales.shape
    words = np.ascontiguousarray(words).reshape(g, 128, n, -1)
    if fmt == "e4m3":
        vals = words.view(ml_dtypes.float8_e4m3fn).astype(np.float64)
    else:
        nib = np.empty((g, 128, n, 4), np.uint8)
        nib[..., 0::2] = words & 0xF
        nib[..., 1::2] = words >> 4
        vals = E2M1[nib]
    vals = vals * np.repeat(np.exp2(scales.astype(np.float64) - 127.0), 8, axis=1)[..., None]
    return vals.transpose(0, 1, 3, 2).reshape(g * 512, n)


def sigm(f):
    return 1.0 / (1.0 + np.exp(-np.maximum(f, -700.0)))


K, N, T, J = 512, 512, 2048, 1024


def setup_inputs():
    n = np.random.standard_normal
    s = mx_kscale(K)[:, None]
    p_tab = pack_weight(n((K, T)) * s, "e4m3")
    p_wa = pack_weight(n((K, N)) / np.sqrt(2 * K) / s, "e2m1")
    p_wb = pack_weight(n((K, N)) / np.sqrt(2 * K) / s, "e2m1")
    p_wc = pack_weight(n((K, N)) / np.sqrt(K) / s, "e2m1")
    return {
        "tab_words": p_tab[0],
        "tab_scales": p_tab[1],
        "wa_words": p_wa[0],
        "wa_scales": p_wa[1],
        "wb_words": p_wb[0],
        "wb_scales": p_wb[1],
        "wc_words": p_wc[0],
        "wc_scales": p_wc[1],
        "wo": (n((K, N)) / np.sqrt(K) / s).astype(np.float32),
        "wgo": np.tile(np.random.uniform(0.5, 2.0, J), (128, 1)).astype(np.float32),
        "offs": striped(np.random.permutation(T)[:J]),
        "offs2": striped(np.random.permutation(T)[:J]),
    }


def reference(tab_words, tab_scales, wa_words, wa_scales, wb_words, wb_scales, wc_words, wc_scales, wo, wgo, offs, offs2):
    idx = unstriped(offs)
    idx2 = unstriped(offs2)
    tab_ = unpack_weight(tab_words, tab_scales, "e4m3")[:, idx]
    tabb_ = unpack_weight(tab_words, tab_scales, "e4m3")[:, idx2]
    wa_ = unpack_weight(wa_words, wa_scales, "e2m1")
    wb_ = unpack_weight(wb_words, wb_scales, "e2m1")
    za = wa_.T @ tabb_ + wb_.T @ tab_
    eta = sigm(za)
    wc_ = unpack_weight(wc_words, wc_scales, "e2m1")
    ms = wc_.T @ tab_
    wo_ = mxq(f64(wo), 0, "e4m3")
    ow = wo_.T @ tabb_
    out = np.zeros((N, T))
    out[:, idx2] = f64(wgo)[0] * (ow + eta * ms)
    return out

@@ -1,0 +1,182 @@
+from contextlib import ExitStack
+
+import concourse.mybir as mybir
+from concourse.masks import make_identity
+
+K, N, T, J = 512, 512, 2048, 1024
+FLOPS = 2 * 4 * K * N * J
+
+F32 = mybir.dt.float32
+BF16 = mybir.dt.bfloat16
+I32 = mybir.dt.int32
+U32 = mybir.dt.uint32
+U16 = mybir.dt.uint16
+U8 = mybir.dt.uint8
+FP8X4 = mybir.dt.float8_e4m3fn_x4
+FP4X4 = mybir.dt.float4_e2m1fn_x4
+ACT = mybir.ActivationFunctionType
+MULT = mybir.AluOpType.mult
+
+P = 128
+PACK = 4
+ROW_BLOCKS = N // P
+CHUNK = 256
+CHUNKS = J // CHUNK
+EARLY_ROWS = 2
+PIECES = ((0, 256), (256, 512), (512, 1024))
+
+
+def tile_list_rgg_own_kernel(
+    tc, tab_words, tab_scales, wa_words, wa_scales, wb_words, wb_scales, wc_words, wc_scales, wo, wgo, offs, offs2, out
+):
+    nc = tc.nc
+    with ExitStack() as ctx:
+        keep = ctx.enter_context(tc.tile_pool(name="keep", bufs=1))
+        reuse = ctx.enter_context(tc.tile_pool(name="reuse", bufs=1))
+        work = ctx.enter_context(tc.tile_pool(name="work", bufs=3))
+        psum = ctx.enter_context(tc.psum_pool(name="psum", bufs=2))
+
+        src_list = keep.tile([P, J // 16], U16, name="src_list")
+        dst_list = keep.tile([P, J // 16], U16, name="dst_list")
+        table = keep.tile([P, T], I32, name="table", align_bytes=64)
+        table_scales = keep.tile([P, T], U8, name="table_scales", align_bytes=64)
+        w_scales = keep.tile([P, 3 * N], U8, name="w_scales", align_bytes=64)
+
+        nc.gpsimd.memset(table_scales[:].bitcast(I32), 0)
+        nc.vector.memset(w_scales[:].bitcast(I32), 0)
+        wgo_rows = keep.tile([P, P], F32, name="wgo_rows")
+        nc.vector.memset(wgo_rows[:], 0.0)
+
+        nc.sync.dma_start(dst_list[:], offs2)
+        nc.sync.dma_start(src_list[:], offs)
+        nc.sync.dma_start(table[:], tab_words[0].rearrange("p t i -> p (t i)").bitcast(I32))
+        for q in range(4):
+            nc.sync.dma_start(
+                table_scales[32 * q : 32 * q + 4, :].bitcast(I32), tab_scales[0, 4 * q : 4 * q + 4, :].bitcast(I32)
+            )
+        for i, scales in enumerate((wa_scales, wb_scales, wc_scales)):
+            nc.sync.dma_start(w_scales[0:16, i * N : (i + 1) * N].bitcast(I32), scales[0].bitcast(I32))
+        w4 = [keep.tile([P, 2 * N], U8, name=name, align_bytes=64) for name in ("wa", "wb", "wc")]
+        for q in range(1, 4):
+            nc.scalar.dma_start(
+                w_scales[32 * q : 32 * q + 4, :].bitcast(I32), w_scales[4 * q : 4 * q + 4, :].bitcast(I32)
+            )
+        half = N // 2
+        wo_raw = keep.tile([P, 2, PACK, half], F32, name="wo_raw", tag="wo_raw_then_page", align_bytes=64)
+        wo_rows = wo.rearrange("(p i) n -> p i n", i=PACK)
+        nc.sync.dma_start(wo_raw[:, 0], wo_rows[:, :, 0:half])
+        nc.sync.dma_start(w4[0][:].bitcast(I32), wa_words[0].bitcast(I32))
+        nc.sync.dma_start(w4[1][:].bitcast(I32), wb_words[0].bitcast(I32))
+        nc.sync.dma_start(wo_raw[:, 1], wo_rows[:, :, half:N])
+        nc.sync.dma_start(w4[2][:].bitcast(I32), wc_words[0].bitcast(I32))
+
+        ident = keep.tile([P, P], F32, name="ident")
+        make_identity(nc, ident[:])
+
+        nc.gpsimd.dma_start(wgo_rows[0 : J // P, :], wgo[0].rearrange("(b j) -> b j", j=P))
+        wgo_bank = psum.tile([P, ROW_BLOCKS, P], F32, name="wgo_bank", tag="turned")
+        nc.tensor.transpose(wgo_bank[:, 0, :], wgo_rows[:], ident[:])
+        wgo_col = keep.tile([P, J // P], F32, name="wgo_col")
+        nc.scalar.copy(wgo_col[:], wgo_bank[:, 0, 0 : J // P])
+
+        pages = []
+        for r in range(ROW_BLOCKS - 1):
+            page = keep.tile([P, T], F32, name="page%d" % r)
+            nc.vector.memset(page[:], 0.0)
+            pages.append(page)
+        warm = keep.tile([P, 1], F32, name="warm")
+        nc.scalar.activation(warm[:], pages[0][:, 0:1], ACT.Sigmoid)
+
+        grouped = reuse.tile([P, N, PACK], BF16, name="grouped", align_bytes=64, offset=0)
+        for h in range(2):
+            nc.scalar.copy(
+                grouped[:, h * half : (h + 1) * half, :].rearrange("p (c u) i -> p c i u", u=4),
+                wo_raw[:, h].rearrange("p i (c u) -> p c i u", u=4),
+            )
+        page = keep.tile([P, T], F32, name="page3", tag="wo_raw_then_page", align_bytes=64)
+        nc.gpsimd.memset(page[:], 0.0)
+        pages.append(page)
+
+        wo_codes = keep.tile([P, N], U32, name="wo_codes", align_bytes=64)
+        wo_scales = keep.tile([P, N], U8, name="wo_scales", align_bytes=64)
+
+        def gather(c):
+            cols = slice(c * CHUNK // 16, (c + 1) * CHUNK // 16)
+            got = []
+            slots = ((4096, 5376), (8192, 9472), (12288, 0), (1280, 2560))[c]
+            for name, lst, at in (("dst", dst_list, slots[0]), ("src", src_list, slots[1])):
+                words = reuse.tile([P, CHUNK], U32, name="%s_words%d" % (name, c), align_bytes=64, offset=at)
+                scales = reuse.tile([P, CHUNK], U8, name="%s_scales%d" % (name, c), align_bytes=64, offset=at + 1024)
+                nc.vector.tensor_copy(words[:], table[:].bitcast(U32).indirect(lst[:, cols]))
+                nc.vector.tensor_copy(scales[:], table_scales[:].indirect(lst[:, cols]))
+                got.append((words, scales))
+            return got
+
+        def mx(bank, side, cols, rhs, rhs_scale, start, stop):
+            words, scales = side
+            nc.tensor.matmul_mx(
+                out=bank[:], lhsT=words[:, cols].bitcast(FP8X4), lhsT_scale=scales[:, cols],
+                rhs=rhs, rhs_scale=rhs_scale, start=start, stop=stop,
+            )
+
+        def products(b, got):
+            dst, src = got
+            cols = slice((b * P) % CHUNK, (b * P) % CHUNK + P)
+            za = psum.tile([P, N], F32, name="za")
+            ms = psum.tile([P, N], F32, name="ms")
+            ow = psum.tile([P, N], F32, name="ow")
+            mx(za, dst, cols, w4[0][:].bitcast(FP4X4), w_scales[:, 0:N], True, False)
+            mx(za, src, cols, w4[1][:].bitcast(FP4X4), w_scales[:, N : 2 * N], False, True)
+            mx(ms, src, cols, w4[2][:].bitcast(FP4X4), w_scales[:, 2 * N : 3 * N], True, True)
+            mx(ow, dst, cols, wo_codes[:].bitcast(FP8X4), wo_scales[:], True, True)
+            eta = work.tile([P, N], F32, name="eta")
+            msw = work.tile([P, N], F32, name="msw")
+            oww = work.tile([P, N], F32, name="oww")
+            gated = work.tile([P, N], F32, name="gated")
+            nc.scalar.activation(eta[:], za[:], ACT.Sigmoid)
+            nc.scalar.activation(msw[:], ms[:], ACT.Copy, scale=wgo_col[:, b : b + 1])
+            nc.gpsimd.tensor_tensor(gated[:], eta[:], msw[:], MULT)
+            nc.scalar.activation(oww[:], ow[:], ACT.Copy, scale=wgo_col[:, b : b + 1])
+            return oww, gated
+
+        stages = [keep.tile([P, ROW_BLOCKS, hi - lo], F32, name="stage%d" % lo) for lo, hi in PIECES]
+
+        def turn(b, terms):
+            oww, gated = terms
+            bank = psum.tile([P, ROW_BLOCKS, P], F32, name="turned", tag="turned")
+            for r in range(ROW_BLOCKS):
+                rows = slice(r * P, (r + 1) * P)
+                nc.tensor.matmul(bank[:, r, :], oww[:, rows], ident[:], start=True, stop=False, is_transpose=True)
+                nc.tensor.matmul(bank[:, r, :], gated[:, rows], ident[:], start=False, stop=True, is_transpose=True)
+            for (lo, hi), stage in zip(PIECES, stages):
+                if lo <= b * P < hi:
+                    nc.scalar.copy(stage[:, :, b * P - lo : b * P - lo + P], bank[:])
+                if lo <= b * P < hi and (b + 1) * P % CHUNK == 0:
+                    upto = (b + 1) * P
+                    for r in range(ROW_BLOCKS):
+                        if r < EARLY_ROWS:
+                            first = upto - CHUNK
+                        elif upto == hi:
+                            first = lo
+                        else:
+                            continue
+                        nc.vector.tensor_copy(
+                            pages[r][:].indirect(dst_list[:, first // 16 : upto // 16]),
+                            stage[:, r, first - lo : upto - lo],
+                        )
+                        if upto == J:
+                            nc.sync.dma_start(out[r * P : (r + 1) * P, :], pages[r][:])
+
+        gots = [gather(0), gather(1)]
+        nc.vector.quantize_mx(
+            out=wo_codes[:].bitcast(FP8X4), scales=wo_scales[:], in_=grouped[:].rearrange("p n i -> p (n i)")
+        )
+        gots.extend([gather(2), gather(3)])
+        per_chunk = CHUNK // P
+        pending = None
+        for b in range(J // P):
+            terms = products(b, gots[b // per_chunk])
+            if pending is not None:
+                turn(b - 1, pending)
+            pending = terms
+        turn(J // P - 1, pending)

@@ -22,8 +22,13 @@ PACK = 4
 ROW_BLOCKS = N // P
 CHUNK = 256
 CHUNKS = J // CHUNK
-EARLY_ROWS = 2
-PIECES = ((0, 256), (256, 512), (512, 1024))
+HALF = J // 2
+PIECES = (
+    ((0, 256), (256, 512), (512, 768), (768, 1024)),
+    ((0, 256), (256, 512), (512, 768), (768, 1024)),
+    ((0, 256), (256, 512), (512, 768), (768, 1024)),
+    ((0, 256), (256, 512), (512, 1024)),
+)
 
 
 def tile_list_rgg_own_kernel(
@@ -33,7 +38,7 @@ def tile_list_rgg_own_kernel(
     with ExitStack() as ctx:
         keep = ctx.enter_context(tc.tile_pool(name="keep", bufs=1))
         reuse = ctx.enter_context(tc.tile_pool(name="reuse", bufs=1))
-        work = ctx.enter_context(tc.tile_pool(name="work", bufs=3))
+        work = ctx.enter_context(tc.tile_pool(name="work", bufs=4))
         psum = ctx.enter_context(tc.psum_pool(name="psum", bufs=2))
 
         src_list = keep.tile([P, J // 16], U16, name="src_list")
@@ -49,11 +54,11 @@ def tile_list_rgg_own_kernel(
 
         nc.sync.dma_start(dst_list[:], offs2)
         nc.sync.dma_start(src_list[:], offs)
-        nc.sync.dma_start(table[:], tab_words[0].rearrange("p t i -> p (t i)").bitcast(I32))
         for q in range(4):
             nc.sync.dma_start(
                 table_scales[32 * q : 32 * q + 4, :].bitcast(I32), tab_scales[0, 4 * q : 4 * q + 4, :].bitcast(I32)
             )
+        nc.sync.dma_start(table[:], tab_words[0].rearrange("p t i -> p (t i)").bitcast(I32))
         for i, scales in enumerate((wa_scales, wb_scales, wc_scales)):
             nc.sync.dma_start(w_scales[0:16, i * N : (i + 1) * N].bitcast(I32), scales[0].bitcast(I32))
         w4 = [keep.tile([P, 2 * N], U8, name=name, align_bytes=64) for name in ("wa", "wb", "wc")]
@@ -82,7 +87,7 @@ def tile_list_rgg_own_kernel(
         pages = []
         for r in range(ROW_BLOCKS - 1):
             page = keep.tile([P, T], F32, name="page%d" % r)
-            nc.vector.memset(page[:], 0.0)
+            (nc.vector if r == 0 else nc.gpsimd).memset(page[:], 0.0)
             pages.append(page)
         warm = keep.tile([P, 1], F32, name="warm")
         nc.scalar.activation(warm[:], pages[0][:, 0:1], ACT.Sigmoid)
@@ -93,90 +98,86 @@ def tile_list_rgg_own_kernel(
                 grouped[:, h * half : (h + 1) * half, :].rearrange("p (c u) i -> p c i u", u=4),
                 wo_raw[:, h].rearrange("p i (c u) -> p c i u", u=4),
             )
-        page = keep.tile([P, T], F32, name="page3", tag="wo_raw_then_page", align_bytes=64)
-        nc.gpsimd.memset(page[:], 0.0)
-        pages.append(page)
 
         wo_codes = keep.tile([P, N], U32, name="wo_codes", align_bytes=64)
         wo_scales = keep.tile([P, N], U8, name="wo_scales", align_bytes=64)
 
-        def gather(c):
-            cols = slice(c * CHUNK // 16, (c + 1) * CHUNK // 16)
-            got = []
-            slots = ((4096, 5376), (8192, 9472), (12288, 0), (1280, 2560))[c]
-            for name, lst, at in (("dst", dst_list, slots[0]), ("src", src_list, slots[1])):
-                words = reuse.tile([P, CHUNK], U32, name="%s_words%d" % (name, c), align_bytes=64, offset=at)
-                scales = reuse.tile([P, CHUNK], U8, name="%s_scales%d" % (name, c), align_bytes=64, offset=at + 1024)
-                nc.vector.tensor_copy(words[:], table[:].bitcast(U32).indirect(lst[:, cols]))
-                nc.vector.tensor_copy(scales[:], table_scales[:].indirect(lst[:, cols]))
-                got.append((words, scales))
-            return got
+        lists = {"dst": dst_list, "src": src_list}
+        words = {}
+        scales = {}
 
-        def mx(bank, side, cols, rhs, rhs_scale, start, stop):
-            words, scales = side
+        def gather_words(side, c, at):
+            got = reuse.tile([P, CHUNK], U32, name="%s_words%d" % (side, c), align_bytes=64, offset=at)
+            cols = slice(c * CHUNK // 16, (c + 1) * CHUNK // 16)
+            nc.vector.tensor_copy(got[:], table[:].bitcast(U32).indirect(lists[side][:, cols]))
+            words[side, c] = got
+
+        def gather_scales(side, h, at):
+            got = reuse.tile([P, HALF], U8, name="%s_scales%d" % (side, h), align_bytes=64, offset=at)
+            cols = slice(h * HALF // 16, (h + 1) * HALF // 16)
+            nc.vector.tensor_copy(got[:], table_scales[:].indirect(lists[side][:, cols]))
+            scales[side, h] = got
+
+        def mx(bank, side, b, rhs, rhs_scale, start, stop):
+            c, in_chunk = divmod(b * P, CHUNK)
+            h, in_half = divmod(b * P, HALF)
             nc.tensor.matmul_mx(
-                out=bank[:], lhsT=words[:, cols].bitcast(FP8X4), lhsT_scale=scales[:, cols],
+                out=bank[:], lhsT=words[side, c][:, in_chunk : in_chunk + P].bitcast(FP8X4),
+                lhsT_scale=scales[side, h][:, in_half : in_half + P],
                 rhs=rhs, rhs_scale=rhs_scale, start=start, stop=stop,
             )
 
-        def products(b, got):
-            dst, src = got
-            cols = slice((b * P) % CHUNK, (b * P) % CHUNK + P)
+        def products(b):
             za = psum.tile([P, N], F32, name="za")
             ms = psum.tile([P, N], F32, name="ms")
             ow = psum.tile([P, N], F32, name="ow")
-            mx(za, dst, cols, w4[0][:].bitcast(FP4X4), w_scales[:, 0:N], True, False)
-            mx(za, src, cols, w4[1][:].bitcast(FP4X4), w_scales[:, N : 2 * N], False, True)
-            mx(ms, src, cols, w4[2][:].bitcast(FP4X4), w_scales[:, 2 * N : 3 * N], True, True)
-            mx(ow, dst, cols, wo_codes[:].bitcast(FP8X4), wo_scales[:], True, True)
+            mx(za, "dst", b, w4[0][:].bitcast(FP4X4), w_scales[:, 0:N], True, False)
+            mx(za, "src", b, w4[1][:].bitcast(FP4X4), w_scales[:, N : 2 * N], False, True)
+            mx(ms, "src", b, w4[2][:].bitcast(FP4X4), w_scales[:, 2 * N : 3 * N], True, True)
+            mx(ow, "dst", b, wo_codes[:].bitcast(FP8X4), wo_scales[:], True, True)
             eta = work.tile([P, N], F32, name="eta")
-            msw = work.tile([P, N], F32, name="msw")
-            oww = work.tile([P, N], F32, name="oww")
+            message = work.tile([P, N], F32, name="message")
+            own = work.tile([P, N], F32, name="own")
             gated = work.tile([P, N], F32, name="gated")
             nc.scalar.activation(eta[:], za[:], ACT.Sigmoid)
-            nc.scalar.activation(msw[:], ms[:], ACT.Copy, scale=wgo_col[:, b : b + 1])
-            nc.gpsimd.tensor_tensor(gated[:], eta[:], msw[:], MULT)
-            nc.scalar.activation(oww[:], ow[:], ACT.Copy, scale=wgo_col[:, b : b + 1])
-            return oww, gated
+            nc.scalar.activation(message[:], ms[:], ACT.Copy, scale=wgo_col[:, b : b + 1])
+            nc.gpsimd.tensor_tensor(gated[:], eta[:], message[:], MULT)
+            nc.scalar.activation(own[:], ow[:], ACT.Copy, scale=wgo_col[:, b : b + 1])
+            return own, gated
 
-        stages = [keep.tile([P, ROW_BLOCKS, hi - lo], F32, name="stage%d" % lo) for lo, hi in PIECES]
+        stage = keep.tile([P, ROW_BLOCKS, J], F32, name="stage")
 
-        def turn(b, terms):
-            oww, gated = terms
+        def turn(b):
+            own, gated = terms[b]
             bank = psum.tile([P, ROW_BLOCKS, P], F32, name="turned", tag="turned")
             for r in range(ROW_BLOCKS):
                 rows = slice(r * P, (r + 1) * P)
-                nc.tensor.matmul(bank[:, r, :], oww[:, rows], ident[:], start=True, stop=False, is_transpose=True)
+                nc.tensor.matmul(bank[:, r, :], own[:, rows], ident[:], start=True, stop=False, is_transpose=True)
                 nc.tensor.matmul(bank[:, r, :], gated[:, rows], ident[:], start=False, stop=True, is_transpose=True)
-            for (lo, hi), stage in zip(PIECES, stages):
-                if lo <= b * P < hi:
-                    nc.scalar.copy(stage[:, :, b * P - lo : b * P - lo + P], bank[:])
-                if lo <= b * P < hi and (b + 1) * P % CHUNK == 0:
-                    upto = (b + 1) * P
-                    for r in range(ROW_BLOCKS):
-                        if r < EARLY_ROWS:
-                            first = upto - CHUNK
-                        elif upto == hi:
-                            first = lo
-                        else:
-                            continue
-                        nc.vector.tensor_copy(
-                            pages[r][:].indirect(dst_list[:, first // 16 : upto // 16]),
-                            stage[:, r, first - lo : upto - lo],
-                        )
-                        if upto == J:
+            nc.scalar.copy(stage[:, :, b * P : (b + 1) * P], bank[:])
+            for r in range(ROW_BLOCKS):
+                for lo, hi in PIECES[r]:
+                    if hi == (b + 1) * P:
+                        nc.vector.tensor_copy(pages[r][:].indirect(dst_list[:, lo // 16 : hi // 16]), stage[:, r, lo:hi])
+                        if hi == J:
                             nc.sync.dma_start(out[r * P : (r + 1) * P, :], pages[r][:])
 
-        gots = [gather(0), gather(1)]
+        gather_scales("dst", 0, 4096)
+        gather_scales("src", 0, 4608)
+        for c in range(3):
+            gather_words("dst", c, 5120 + 2048 * c)
+            gather_words("src", c, 6144 + 2048 * c)
         nc.vector.quantize_mx(
             out=wo_codes[:].bitcast(FP8X4), scales=wo_scales[:], in_=grouped[:].rearrange("p n i -> p (n i)")
         )
-        gots.extend([gather(2), gather(3)])
-        per_chunk = CHUNK // P
-        pending = None
+        gather_scales("dst", 1, 0)
+        gather_scales("src", 1, 512)
+        gather_words("dst", 3, 1024)
+        gather_words("src", 3, 2048)
+        page = keep.tile([P, T], F32, name="page3", tag="wo_raw_then_page", align_bytes=64)
+        nc.vector.memset(page[:], 0.0)
+        pages.append(page)
+        terms = []
         for b in range(J // P):
-            terms = products(b, gots[b // per_chunk])
-            if pending is not None:
-                turn(b - 1, pending)
-            pending = terms
-        turn(J // P - 1, pending)
+            terms.append(products(b))
+            turn(b)

@@ -19,16 +19,9 @@ MULT = mybir.AluOpType.mult
 
 P = 128
 PACK = 4
-ROW_BLOCKS = N // P
-CHUNK = 256
-CHUNKS = J // CHUNK
-HALF = J // 2
-PIECES = (
-    ((0, 256), (256, 512), (512, 768), (768, 1024)),
-    ((0, 256), (256, 512), (512, 768), (768, 1024)),
-    ((0, 256), (256, 512), (512, 768), (768, 1024)),
-    ((0, 256), (256, 512), (512, 1024)),
-)
+HALF_J = J // 2
+HALF_N = N // 2
+PAGES = 3
 
 
 def tile_list_rgg_own_kernel(
@@ -38,7 +31,7 @@ def tile_list_rgg_own_kernel(
     with ExitStack() as ctx:
         keep = ctx.enter_context(tc.tile_pool(name="keep", bufs=1))
         reuse = ctx.enter_context(tc.tile_pool(name="reuse", bufs=1))
-        work = ctx.enter_context(tc.tile_pool(name="work", bufs=4))
+        work = ctx.enter_context(tc.tile_pool(name="work", bufs=3))
         psum = ctx.enter_context(tc.psum_pool(name="psum", bufs=2))
 
         src_list = keep.tile([P, J // 16], U16, name="src_list")
@@ -46,138 +39,142 @@ def tile_list_rgg_own_kernel(
         table = keep.tile([P, T], I32, name="table", align_bytes=64)
         table_scales = keep.tile([P, T], U8, name="table_scales", align_bytes=64)
         w_scales = keep.tile([P, 3 * N], U8, name="w_scales", align_bytes=64)
+        wgo_rows = keep.tile([P, P], F32, name="wgo_rows")
+        pages = [keep.tile([P, T], F32, name="page%d" % i) for i in range(PAGES - 1)]
 
         nc.gpsimd.memset(table_scales[:].bitcast(I32), 0)
+        ident = keep.tile([P, P], F32, name="ident")
+        make_identity(nc, ident[:])
         nc.vector.memset(w_scales[:].bitcast(I32), 0)
-        wgo_rows = keep.tile([P, P], F32, name="wgo_rows")
         nc.vector.memset(wgo_rows[:], 0.0)
+        for page in pages:
+            nc.vector.memset(page[:], 0.0)
 
         nc.sync.dma_start(dst_list[:], offs2)
-        nc.sync.dma_start(src_list[:], offs)
         for q in range(4):
             nc.sync.dma_start(
                 table_scales[32 * q : 32 * q + 4, :].bitcast(I32), tab_scales[0, 4 * q : 4 * q + 4, :].bitcast(I32)
             )
+        nc.sync.dma_start(src_list[:], offs)
         nc.sync.dma_start(table[:], tab_words[0].rearrange("p t i -> p (t i)").bitcast(I32))
         for i, scales in enumerate((wa_scales, wb_scales, wc_scales)):
             nc.sync.dma_start(w_scales[0:16, i * N : (i + 1) * N].bitcast(I32), scales[0].bitcast(I32))
-        w4 = [keep.tile([P, 2 * N], U8, name=name, align_bytes=64) for name in ("wa", "wb", "wc")]
         for q in range(1, 4):
             nc.scalar.dma_start(
                 w_scales[32 * q : 32 * q + 4, :].bitcast(I32), w_scales[4 * q : 4 * q + 4, :].bitcast(I32)
             )
-        half = N // 2
-        wo_raw = keep.tile([P, 2, PACK, half], F32, name="wo_raw", tag="wo_raw_then_page", align_bytes=64)
+        w4 = [keep.tile([P, 2 * N], U8, name=name, align_bytes=64) for name in ("wa", "wb", "wc")]
+        wo_raw = [keep.tile([P, PACK, HALF_N], F32, name="wo_raw%d" % s) for s in range(2)]
         wo_rows = wo.rearrange("(p i) n -> p i n", i=PACK)
-        nc.sync.dma_start(wo_raw[:, 0], wo_rows[:, :, 0:half])
+        nc.sync.dma_start(wo_raw[0][:], wo_rows[:, :, 0:HALF_N])
         nc.sync.dma_start(w4[0][:].bitcast(I32), wa_words[0].bitcast(I32))
         nc.sync.dma_start(w4[1][:].bitcast(I32), wb_words[0].bitcast(I32))
-        nc.sync.dma_start(wo_raw[:, 1], wo_rows[:, :, half:N])
         nc.sync.dma_start(w4[2][:].bitcast(I32), wc_words[0].bitcast(I32))
-
-        ident = keep.tile([P, P], F32, name="ident")
-        make_identity(nc, ident[:])
-
-        nc.gpsimd.dma_start(wgo_rows[0 : J // P, :], wgo[0].rearrange("(b j) -> b j", j=P))
-        wgo_bank = psum.tile([P, ROW_BLOCKS, P], F32, name="wgo_bank", tag="turned")
-        nc.tensor.transpose(wgo_bank[:, 0, :], wgo_rows[:], ident[:])
-        wgo_col = keep.tile([P, J // P], F32, name="wgo_col")
-        nc.scalar.copy(wgo_col[:], wgo_bank[:, 0, 0 : J // P])
-
-        pages = []
-        for r in range(ROW_BLOCKS - 1):
-            page = keep.tile([P, T], F32, name="page%d" % r)
-            (nc.vector if r == 0 else nc.gpsimd).memset(page[:], 0.0)
-            pages.append(page)
-        warm = keep.tile([P, 1], F32, name="warm")
-        nc.scalar.activation(warm[:], pages[0][:, 0:1], ACT.Sigmoid)
-
-        grouped = reuse.tile([P, N, PACK], BF16, name="grouped", align_bytes=64, offset=0)
-        for h in range(2):
-            nc.scalar.copy(
-                grouped[:, h * half : (h + 1) * half, :].rearrange("p (c u) i -> p c i u", u=4),
-                wo_raw[:, h].rearrange("p i (c u) -> p c i u", u=4),
-            )
-
-        wo_codes = keep.tile([P, N], U32, name="wo_codes", align_bytes=64)
-        wo_scales = keep.tile([P, N], U8, name="wo_scales", align_bytes=64)
+        nc.sync.dma_start(wgo_rows[0 : J // P, :], wgo[0].rearrange("(b j) -> b j", j=P))
+        nc.sync.dma_start(wo_raw[1][:], wo_rows[:, :, HALF_N:N])
 
         lists = {"dst": dst_list, "src": src_list}
         words = {}
         scales = {}
 
-        def gather_words(side, c, at):
-            got = reuse.tile([P, CHUNK], U32, name="%s_words%d" % (side, c), align_bytes=64, offset=at)
-            cols = slice(c * CHUNK // 16, (c + 1) * CHUNK // 16)
-            nc.vector.tensor_copy(got[:], table[:].bitcast(U32).indirect(lists[side][:, cols]))
-            words[side, c] = got
+        def gather(store, window, dtype, side, lo, hi, at):
+            got = reuse.tile([P, hi - lo], dtype, name="%s_%d" % (side, at), align_bytes=64, offset=at)
+            nc.vector.tensor_copy(got[:], window.indirect(lists[side][:, lo // 16 : hi // 16]))
+            for b in range(lo // P, hi // P):
+                store[side, b] = got[:, b * P - lo : (b + 1) * P - lo]
 
-        def gather_scales(side, h, at):
-            got = reuse.tile([P, HALF], U8, name="%s_scales%d" % (side, h), align_bytes=64, offset=at)
-            cols = slice(h * HALF // 16, (h + 1) * HALF // 16)
-            nc.vector.tensor_copy(got[:], table_scales[:].indirect(lists[side][:, cols]))
-            scales[side, h] = got
+        def gather_words(side, lo, hi, at):
+            gather(words, table[:].bitcast(U32), U32, side, lo, hi, at)
+
+        def gather_scales(side, lo, hi, at):
+            gather(scales, table_scales[:], U8, side, lo, hi, at)
+
+        wo_codes = []
+        wo_scales = []
+
+        def quantise_wo(s, at):
+            grouped = reuse.tile([P, HALF_N, PACK], BF16, name="grouped%d" % s, align_bytes=64, offset=at)
+            nc.scalar.copy(
+                grouped[:].rearrange("p (c u) i -> p c i u", u=4), wo_raw[s][:].rearrange("p i (c u) -> p c i u", u=4)
+            )
+            codes = keep.tile([P, HALF_N], U32, name="wo_codes%d" % s, align_bytes=64)
+            plane = keep.tile([P, HALF_N], U8, name="wo_scales%d" % s, align_bytes=64)
+            nc.vector.quantize_mx(
+                out=codes[:].bitcast(FP8X4), scales=plane[:], in_=grouped[:].rearrange("p n i -> p (n i)")
+            )
+            wo_codes.append(codes)
+            wo_scales.append(plane)
 
         def mx(bank, side, b, rhs, rhs_scale, start, stop):
-            c, in_chunk = divmod(b * P, CHUNK)
-            h, in_half = divmod(b * P, HALF)
             nc.tensor.matmul_mx(
-                out=bank[:], lhsT=words[side, c][:, in_chunk : in_chunk + P].bitcast(FP8X4),
-                lhsT_scale=scales[side, h][:, in_half : in_half + P],
+                out=bank, lhsT=words[side, b].bitcast(FP8X4), lhsT_scale=scales[side, b],
                 rhs=rhs, rhs_scale=rhs_scale, start=start, stop=stop,
             )
 
-        def products(b):
-            za = psum.tile([P, N], F32, name="za")
-            ms = psum.tile([P, N], F32, name="ms")
-            ow = psum.tile([P, N], F32, name="ow")
-            mx(za, "dst", b, w4[0][:].bitcast(FP4X4), w_scales[:, 0:N], True, False)
-            mx(za, "src", b, w4[1][:].bitcast(FP4X4), w_scales[:, N : 2 * N], False, True)
-            mx(ms, "src", b, w4[2][:].bitcast(FP4X4), w_scales[:, 2 * N : 3 * N], True, True)
-            mx(ow, "dst", b, wo_codes[:].bitcast(FP8X4), wo_scales[:], True, True)
-            eta = work.tile([P, N], F32, name="eta")
-            message = work.tile([P, N], F32, name="message")
-            own = work.tile([P, N], F32, name="own")
-            gated = work.tile([P, N], F32, name="gated")
-            nc.scalar.activation(eta[:], za[:], ACT.Sigmoid)
-            nc.scalar.activation(message[:], ms[:], ACT.Copy, scale=wgo_col[:, b : b + 1])
-            nc.gpsimd.tensor_tensor(gated[:], eta[:], message[:], MULT)
-            nc.scalar.activation(own[:], ow[:], ACT.Copy, scale=wgo_col[:, b : b + 1])
-            return own, gated
+        def fp4(i, r):
+            return w4[i][:, 2 * r * P : 2 * (r + 1) * P].bitcast(FP4X4), w_scales[:, i * N + r * P : i * N + (r + 1) * P]
 
-        stage = keep.tile([P, ROW_BLOCKS, J], F32, name="stage")
+        def unit(r, b_lo, b_hi, last, eta=None):
+            n = b_hi - b_lo
+            za = psum.tile([P, 4, P], F32, name="za")
+            ms = psum.tile([P, 4, P], F32, name="ms")
+            ow = psum.tile([P, 4, P], F32, name="ow")
+            s, in_half = divmod(r * P, HALF_N)
+            for i in range(n):
+                mx(za[:, i, :], "dst", b_lo + i, *fp4(0, r), True, False)
+                mx(za[:, i, :], "src", b_lo + i, *fp4(1, r), False, True)
+            for i in range(n):
+                mx(ms[:, i, :], "src", b_lo + i, *fp4(2, r), True, True)
+            for i in range(n):
+                cols = slice(in_half, in_half + P)
+                mx(ow[:, i, :], "dst", b_lo + i, wo_codes[s][:, cols].bitcast(FP8X4), wo_scales[s][:, cols], True, True)
+            if eta is None:
+                eta = work.tile([P, 4, P], F32, name="eta")
+            message = work.tile([P, 4, P], F32, name="message")
+            own = work.tile([P, 4, P], F32, name="own")
+            gated = work.tile([P, 4, P], F32, name="gated")
+            nc.scalar.activation(eta[:, 0:n, :], za[:, 0:n, :], ACT.Sigmoid)
+            for i in range(n):
+                nc.scalar.activation(message[:, i, :], ms[:, i, :], ACT.Copy, scale=wgo_col[:, b_lo + i : b_lo + i + 1])
+            nc.gpsimd.tensor_tensor(gated[:, 0:n, :], eta[:, 0:n, :], message[:, 0:n, :], MULT)
+            for i in range(n):
+                nc.scalar.activation(own[:, i, :], ow[:, i, :], ACT.Copy, scale=wgo_col[:, b_lo + i : b_lo + i + 1])
+            bank = psum.tile([P, 4, P], F32, name="turned", tag="turned")
+            for i in range(n):
+                nc.tensor.matmul(bank[:, i, :], own[:, i, :], ident[:], start=True, stop=False, is_transpose=True)
+                nc.tensor.matmul(bank[:, i, :], gated[:, i, :], ident[:], start=False, stop=True, is_transpose=True)
+            stage = work.tile([P, 4 * P], F32, name="stage")
+            nc.scalar.copy(stage[:, 0 : n * P], bank[:, 0:n, :].rearrange("p i e -> p (i e)"))
+            page = pages[r % PAGES]
+            nc.vector.tensor_copy(page[:].indirect(dst_list[:, b_lo * P // 16 : b_hi * P // 16]), stage[:, 0 : n * P])
+            if last:
+                nc.sync.dma_start(out[r * P : (r + 1) * P, :], page[:])
 
-        def turn(b):
-            own, gated = terms[b]
-            bank = psum.tile([P, ROW_BLOCKS, P], F32, name="turned", tag="turned")
-            for r in range(ROW_BLOCKS):
-                rows = slice(r * P, (r + 1) * P)
-                nc.tensor.matmul(bank[:, r, :], own[:, rows], ident[:], start=True, stop=False, is_transpose=True)
-                nc.tensor.matmul(bank[:, r, :], gated[:, rows], ident[:], start=False, stop=True, is_transpose=True)
-            nc.scalar.copy(stage[:, :, b * P : (b + 1) * P], bank[:])
-            for r in range(ROW_BLOCKS):
-                for lo, hi in PIECES[r]:
-                    if hi == (b + 1) * P:
-                        nc.vector.tensor_copy(pages[r][:].indirect(dst_list[:, lo // 16 : hi // 16]), stage[:, r, lo:hi])
-                        if hi == J:
-                            nc.sync.dma_start(out[r * P : (r + 1) * P, :], pages[r][:])
+        gather_scales("dst", 0, HALF_J, 6144)
+        gather_scales("src", 0, HALF_J, 6656)
+        gather_words("dst", 0, 256, 7168)
+        gather_words("src", 0, 256, 8192)
+        gather_words("dst", 256, 512, 9216)
+        gather_words("src", 256, 512, 10240)
+        quantise_wo(0, 0)
 
-        gather_scales("dst", 0, 4096)
-        gather_scales("src", 0, 4608)
-        for c in range(3):
-            gather_words("dst", c, 5120 + 2048 * c)
-            gather_words("src", c, 6144 + 2048 * c)
-        nc.vector.quantize_mx(
-            out=wo_codes[:].bitcast(FP8X4), scales=wo_scales[:], in_=grouped[:].rearrange("p n i -> p (n i)")
-        )
-        gather_scales("dst", 1, 0)
-        gather_scales("src", 1, 512)
-        gather_words("dst", 3, 1024)
-        gather_words("src", 3, 2048)
-        page = keep.tile([P, T], F32, name="page3", tag="wo_raw_then_page", align_bytes=64)
-        nc.vector.memset(page[:], 0.0)
-        pages.append(page)
-        terms = []
-        for b in range(J // P):
-            terms.append(products(b))
-            turn(b)
+        wgo_bank = psum.tile([P, 4, P], F32, name="wgo_bank", tag="turned")
+        nc.tensor.transpose(wgo_bank[:, 0, :], wgo_rows[:], ident[:])
+        wgo_col = keep.tile([P, J // P], F32, name="wgo_col")
+        nc.scalar.copy(wgo_col[:], wgo_bank[:, 0, 0 : J // P])
+
+        gather_scales("dst", HALF_J, J, 0)
+        gather_scales("src", HALF_J, J, 512)
+        quantise_wo(1, 3072)
+        gather_words("dst", HALF_J, J, 2048)
+        gather_words("src", HALF_J, J, 4096)
+        unit(0, 0, 2, False)
+        unit(0, 2, 4, False)
+        unit(1, 0, 4, False, keep.tile([P, 4, P], F32, name="eta_early", tag="eta_then_page"))
+        pages.append(keep.tile([P, T], F32, name="page2", tag="eta_then_page"))
+        nc.gpsimd.memset(pages[2][:], 0.0)
+        unit(2, 0, 4, False)
+        for r in range(3):
+            unit(r, 4, 8, True)
+        unit(3, 0, 4, False)
+        unit(3, 4, 8, True)

@@ -50,6 +50,9 @@ def tile_list_rgg_own_kernel(
         for page in pages:
             nc.vector.memset(page[:], 0.0)
 
+        warm = keep.tile([P, 1], F32, name="warm")
+        nc.scalar.activation(warm[:], wgo_rows[:, 0:1], ACT.Sigmoid)
+
         nc.sync.dma_start(dst_list[:], offs2)
         for q in range(4):
             nc.sync.dma_start(

@@ -21,7 +21,7 @@ P = 128
 PACK = 4
 HALF_J = J // 2
 HALF_N = N // 2
-PAGES = 3
+PAGE_OF_ROWS = (0, 1, 2, 0)
 
 
 def tile_list_rgg_own_kernel(
@@ -31,7 +31,7 @@ def tile_list_rgg_own_kernel(
     with ExitStack() as ctx:
         keep = ctx.enter_context(tc.tile_pool(name="keep", bufs=1))
         reuse = ctx.enter_context(tc.tile_pool(name="reuse", bufs=1))
-        work = ctx.enter_context(tc.tile_pool(name="work", bufs=3))
+        work = ctx.enter_context(tc.tile_pool(name="work", bufs=4))
         psum = ctx.enter_context(tc.psum_pool(name="psum", bufs=2))
 
         src_list = keep.tile([P, J // 16], U16, name="src_list")
@@ -40,7 +40,7 @@ def tile_list_rgg_own_kernel(
         table_scales = keep.tile([P, T], U8, name="table_scales", align_bytes=64)
         w_scales = keep.tile([P, 3 * N], U8, name="w_scales", align_bytes=64)
         wgo_rows = keep.tile([P, P], F32, name="wgo_rows")
-        pages = [keep.tile([P, T], F32, name="page%d" % i) for i in range(PAGES - 1)]
+        pages = [keep.tile([P, T], F32, name="page%d" % i) for i in range(2)]
 
         nc.gpsimd.memset(table_scales[:].bitcast(I32), 0)
         ident = keep.tile([P, P], F32, name="ident")
@@ -49,9 +49,8 @@ def tile_list_rgg_own_kernel(
         nc.vector.memset(wgo_rows[:], 0.0)
         for page in pages:
             nc.vector.memset(page[:], 0.0)
-
         warm = keep.tile([P, 1], F32, name="warm")
-        nc.scalar.activation(warm[:], wgo_rows[:, 0:1], ACT.Sigmoid)
+        nc.scalar.activation(warm[32:64, :], wgo_rows[32:64, 0:1], ACT.Sigmoid)
 
         nc.sync.dma_start(dst_list[:], offs2)
         for q in range(4):
@@ -67,14 +66,11 @@ def tile_list_rgg_own_kernel(
                 w_scales[32 * q : 32 * q + 4, :].bitcast(I32), w_scales[4 * q : 4 * q + 4, :].bitcast(I32)
             )
         w4 = [keep.tile([P, 2 * N], U8, name=name, align_bytes=64) for name in ("wa", "wb", "wc")]
-        wo_raw = [keep.tile([P, PACK, HALF_N], F32, name="wo_raw%d" % s) for s in range(2)]
         wo_rows = wo.rearrange("(p i) n -> p i n", i=PACK)
-        nc.sync.dma_start(wo_raw[0][:], wo_rows[:, :, 0:HALF_N])
         nc.sync.dma_start(w4[0][:].bitcast(I32), wa_words[0].bitcast(I32))
         nc.sync.dma_start(w4[1][:].bitcast(I32), wb_words[0].bitcast(I32))
         nc.sync.dma_start(w4[2][:].bitcast(I32), wc_words[0].bitcast(I32))
-        nc.sync.dma_start(wgo_rows[0 : J // P, :], wgo[0].rearrange("(b j) -> b j", j=P))
-        nc.sync.dma_start(wo_raw[1][:], wo_rows[:, :, HALF_N:N])
+        nc.gpsimd.dma_start(wgo_rows[0 : J // P, :], wgo[0].rearrange("(b j) -> b j", j=P))
 
         lists = {"dst": dst_list, "src": src_list}
         words = {}
@@ -96,9 +92,11 @@ def tile_list_rgg_own_kernel(
         wo_scales = []
 
         def quantise_wo(s, at):
+            raw = keep.tile([P, PACK, HALF_N], F32, name="wo_raw")
+            nc.sync.dma_start(raw[:], wo_rows[:, :, s * HALF_N : (s + 1) * HALF_N])
             grouped = reuse.tile([P, HALF_N, PACK], BF16, name="grouped%d" % s, align_bytes=64, offset=at)
             nc.scalar.copy(
-                grouped[:].rearrange("p (c u) i -> p c i u", u=4), wo_raw[s][:].rearrange("p i (c u) -> p c i u", u=4)
+                grouped[:].rearrange("p (c u) i -> p c i u", u=4), raw[:].rearrange("p i (c u) -> p c i u", u=4)
             )
             codes = keep.tile([P, HALF_N], U32, name="wo_codes%d" % s, align_bytes=64)
             plane = keep.tile([P, HALF_N], U8, name="wo_scales%d" % s, align_bytes=64)
@@ -117,41 +115,56 @@ def tile_list_rgg_own_kernel(
         def fp4(i, r):
             return w4[i][:, 2 * r * P : 2 * (r + 1) * P].bitcast(FP4X4), w_scales[:, i * N + r * P : i * N + (r + 1) * P]
 
-        def unit(r, b_lo, b_hi, last, eta=None):
-            n = b_hi - b_lo
+        stage = [keep.tile([P, J], F32, name="stage%d" % r) for r in range(N // P)]
+
+        def unit(runs, eta=None):
+            tiles = [(r, b) for r, b_lo, b_hi in runs for b in range(b_lo, b_hi)]
+            n = len(tiles)
             za = psum.tile([P, 4, P], F32, name="za")
             ms = psum.tile([P, 4, P], F32, name="ms")
             ow = psum.tile([P, 4, P], F32, name="ow")
-            s, in_half = divmod(r * P, HALF_N)
-            for i in range(n):
-                mx(za[:, i, :], "dst", b_lo + i, *fp4(0, r), True, False)
-                mx(za[:, i, :], "src", b_lo + i, *fp4(1, r), False, True)
-            for i in range(n):
-                mx(ms[:, i, :], "src", b_lo + i, *fp4(2, r), True, True)
-            for i in range(n):
-                cols = slice(in_half, in_half + P)
-                mx(ow[:, i, :], "dst", b_lo + i, wo_codes[s][:, cols].bitcast(FP8X4), wo_scales[s][:, cols], True, True)
+            for i, (r, b) in enumerate(tiles):
+                mx(za[:, i, :], "dst", b, *fp4(0, r), True, False)
+                mx(za[:, i, :], "src", b, *fp4(1, r), False, True)
+            for i, (r, b) in enumerate(tiles):
+                mx(ms[:, i, :], "src", b, *fp4(2, r), True, True)
+            for i, (r, b) in enumerate(tiles):
+                s, lo = divmod(r * P, HALF_N)
+                mx(ow[:, i, :], "dst", b, wo_codes[s][:, lo : lo + P].bitcast(FP8X4), wo_scales[s][:, lo : lo + P], True, True)
             if eta is None:
                 eta = work.tile([P, 4, P], F32, name="eta")
             message = work.tile([P, 4, P], F32, name="message")
             own = work.tile([P, 4, P], F32, name="own")
             gated = work.tile([P, 4, P], F32, name="gated")
             nc.scalar.activation(eta[:, 0:n, :], za[:, 0:n, :], ACT.Sigmoid)
-            for i in range(n):
-                nc.scalar.activation(message[:, i, :], ms[:, i, :], ACT.Copy, scale=wgo_col[:, b_lo + i : b_lo + i + 1])
+            for i, (r, b) in enumerate(tiles):
+                nc.scalar.activation(message[:, i, :], ms[:, i, :], ACT.Copy, scale=wgo_col[:, b : b + 1])
             nc.gpsimd.tensor_tensor(gated[:, 0:n, :], eta[:, 0:n, :], message[:, 0:n, :], MULT)
+            for i, (r, b) in enumerate(tiles):
+                nc.scalar.activation(own[:, i, :], ow[:, i, :], ACT.Copy, scale=wgo_col[:, b : b + 1])
+            bank = psum.tile([P, 4 * P], F32, name="turned", tag="turned")
             for i in range(n):
-                nc.scalar.activation(own[:, i, :], ow[:, i, :], ACT.Copy, scale=wgo_col[:, b_lo + i : b_lo + i + 1])
-            bank = psum.tile([P, 4, P], F32, name="turned", tag="turned")
-            for i in range(n):
-                nc.tensor.matmul(bank[:, i, :], own[:, i, :], ident[:], start=True, stop=False, is_transpose=True)
-                nc.tensor.matmul(bank[:, i, :], gated[:, i, :], ident[:], start=False, stop=True, is_transpose=True)
-            stage = work.tile([P, 4 * P], F32, name="stage")
-            nc.scalar.copy(stage[:, 0 : n * P], bank[:, 0:n, :].rearrange("p i e -> p (i e)"))
-            page = pages[r % PAGES]
-            nc.vector.tensor_copy(page[:].indirect(dst_list[:, b_lo * P // 16 : b_hi * P // 16]), stage[:, 0 : n * P])
-            if last:
+                cols = slice(i * P, (i + 1) * P)
+                nc.tensor.matmul(bank[:, cols], own[:, i, :], ident[:], start=True, stop=False, is_transpose=True)
+                nc.tensor.matmul(bank[:, cols], gated[:, i, :], ident[:], start=False, stop=True, is_transpose=True)
+            at = 0
+            for r, b_lo, b_hi in runs:
+                width = (b_hi - b_lo) * P
+                nc.scalar.copy(stage[r][:, b_lo * P : b_hi * P], bank[:, at : at + width])
+                at = at + width
+
+        def scatter(r, b_lo, b_hi):
+            page = pages[PAGE_OF_ROWS[r]]
+            nc.vector.tensor_copy(
+                page[:].indirect(dst_list[:, b_lo * P // 16 : b_hi * P // 16]), stage[r][:, b_lo * P : b_hi * P]
+            )
+            if b_hi == J // P:
                 nc.sync.dma_start(out[r * P : (r + 1) * P, :], page[:])
+
+        wgo_bank = psum.tile([P, 4 * P], F32, name="wgo_bank", tag="turned")
+        nc.tensor.transpose(wgo_bank[:, 0:P], wgo_rows[:], ident[:])
+        wgo_col = keep.tile([P, J // P], F32, name="wgo_col")
+        nc.scalar.copy(wgo_col[:], wgo_bank[:, 0 : J // P])
 
         gather_scales("dst", 0, HALF_J, 6144)
         gather_scales("src", 0, HALF_J, 6656)
@@ -159,25 +172,26 @@ def tile_list_rgg_own_kernel(
         gather_words("src", 0, 256, 8192)
         gather_words("dst", 256, 512, 9216)
         gather_words("src", 256, 512, 10240)
-        quantise_wo(0, 0)
-
-        wgo_bank = psum.tile([P, 4, P], F32, name="wgo_bank", tag="turned")
-        nc.tensor.transpose(wgo_bank[:, 0, :], wgo_rows[:], ident[:])
-        wgo_col = keep.tile([P, J // P], F32, name="wgo_col")
-        nc.scalar.copy(wgo_col[:], wgo_bank[:, 0, 0 : J // P])
-
         gather_scales("dst", HALF_J, J, 0)
-        gather_scales("src", HALF_J, J, 512)
-        quantise_wo(1, 3072)
-        gather_words("dst", HALF_J, J, 2048)
-        gather_words("src", HALF_J, J, 4096)
-        unit(0, 0, 2, False)
-        unit(0, 2, 4, False)
-        unit(1, 0, 4, False, keep.tile([P, 4, P], F32, name="eta_early", tag="eta_then_page"))
-        pages.append(keep.tile([P, T], F32, name="page2", tag="eta_then_page"))
+        quantise_wo(0, 2048)
+        gather_scales("src", HALF_J, J, 2560)
+        gather_words("dst", HALF_J, J, 512)
+        gather_words("src", HALF_J, J, 3072)
+        unit([(0, 0, 2)])
+        scatter(0, 0, 2)
+        unit([(1, 0, 2)])
+        scatter(1, 0, 2)
+        unit([(0, 2, 4), (1, 2, 4)])
+        scatter(0, 2, 4)
+        scatter(1, 2, 4)
+        unit([(0, 4, 8)], reuse.tile([P, 4, P], F32, name="eta_early", align_bytes=64, offset=12288))
+        scatter(0, 4, 8)
+        pages.append(reuse.tile([P, T], F32, name="page2", align_bytes=64, offset=13312))
         nc.gpsimd.memset(pages[2][:], 0.0)
-        unit(2, 0, 4, False)
-        for r in range(3):
-            unit(r, 4, 8, True)
-        unit(3, 0, 4, False)
-        unit(3, 4, 8, True)
+        unit([(1, 4, 8)])
+        scatter(1, 4, 8)
+        quantise_wo(1, 11264)
+        for b_lo in (0, 4):
+            for r in (2, 3):
+                unit([(r, b_lo, b_lo + 4)])
+                scatter(r, b_lo, b_lo + 4)

@@ -43,17 +43,18 @@ def tile_list_rgg_own_kernel(
         pages = [keep.tile([P, T], F32, name="page%d" % i) for i in range(2)]
 
         nc.gpsimd.memset(table_scales[:].bitcast(I32), 0)
+        nc.gpsimd.memset(wgo_rows[:], 0.0)
+        nc.gpsimd.dma_start(wgo_rows[0 : J // P, :], wgo[0].rearrange("(b j) -> b j", j=P))
         ident = keep.tile([P, P], F32, name="ident")
         make_identity(nc, ident[:])
         nc.vector.memset(w_scales[:].bitcast(I32), 0)
-        nc.vector.memset(wgo_rows[:], 0.0)
-        for page in pages:
-            nc.vector.memset(page[:], 0.0)
+        nc.vector.memset(pages[0][:], 0.0)
+        nc.gpsimd.memset(pages[1][:], 0.0)
         warm = keep.tile([P, 1], F32, name="warm")
         nc.scalar.activation(warm[32:64, :], wgo_rows[32:64, 0:1], ACT.Sigmoid)
 
         nc.sync.dma_start(dst_list[:], offs2)
-        for q in range(4):
+        for q in (2, 3, 0, 1):
             nc.sync.dma_start(
                 table_scales[32 * q : 32 * q + 4, :].bitcast(I32), tab_scales[0, 4 * q : 4 * q + 4, :].bitcast(I32)
             )
@@ -70,7 +71,6 @@ def tile_list_rgg_own_kernel(
         nc.sync.dma_start(w4[0][:].bitcast(I32), wa_words[0].bitcast(I32))
         nc.sync.dma_start(w4[1][:].bitcast(I32), wb_words[0].bitcast(I32))
         nc.sync.dma_start(w4[2][:].bitcast(I32), wc_words[0].bitcast(I32))
-        nc.gpsimd.dma_start(wgo_rows[0 : J // P, :], wgo[0].rearrange("(b j) -> b j", j=P))
 
         lists = {"dst": dst_list, "src": src_list}
         words = {}

@@ -92,7 +92,7 @@ def tile_list_rgg_own_kernel(
         wo_scales = []
 
         def quantise_wo(s, at):
-            raw = keep.tile([P, PACK, HALF_N], F32, name="wo_raw")
+            raw = reuse.tile([P, PACK, HALF_N], F32, name="wo_raw%d" % s, align_bytes=64, offset=(23552, 26176)[s])
             nc.sync.dma_start(raw[:], wo_rows[:, :, s * HALF_N : (s + 1) * HALF_N])
             grouped = reuse.tile([P, HALF_N, PACK], BF16, name="grouped%d" % s, align_bytes=64, offset=at)
             nc.scalar.copy(
@@ -174,9 +174,9 @@ def tile_list_rgg_own_kernel(
         gather_words("src", 256, 512, 10240)
         gather_scales("dst", HALF_J, J, 0)
         quantise_wo(0, 2048)
-        gather_scales("src", HALF_J, J, 2560)
-        gather_words("dst", HALF_J, J, 512)
-        gather_words("src", HALF_J, J, 3072)
+        gather_scales("src", HALF_J, J, 23616)
+        gather_words("dst", HALF_J, J, 21568)
+        gather_words("src", HALF_J, J, 24128)
         unit([(0, 0, 2)])
         scatter(0, 0, 2)
         unit([(1, 0, 2)])

@@ -54,8 +54,8 @@ def tile_list_rgg_own_kernel(
         nc.scalar.activation(warm[32:64, :], wgo_rows[32:64, 0:1], ACT.Sigmoid)
 
         nc.sync.dma_start(dst_list[:], offs2)
-        for q in (2, 3, 0, 1):
-            nc.sync.dma_start(
+        for q, queue in ((2, nc.scalar), (0, nc.sync), (3, nc.sync), (1, nc.sync)):
+            queue.dma_start(
                 table_scales[32 * q : 32 * q + 4, :].bitcast(I32), tab_scales[0, 4 * q : 4 * q + 4, :].bitcast(I32)
             )
         nc.sync.dma_start(src_list[:], offs)

@@ -19,9 +19,17 @@ MULT = mybir.AluOpType.mult
 
 P = 128
 PACK = 4
+QUARTER_J = J // 4
 HALF_J = J // 2
 HALF_N = N // 2
 PAGE_OF_ROWS = (0, 1, 2, 0)
+
+RAW_AT = (2048, 5696)
+LATE_DST_WORDS_AT = 64
+LATE_SRC_SCALES_AT = 3136
+LATE_SRC_WORDS_AT = 3648
+SECOND_ROUNDED_AT = 9792
+FOURTH_GATE_AT = 10816
 
 
 def tile_list_rgg_own_kernel(
@@ -39,17 +47,23 @@ def tile_list_rgg_own_kernel(
         table = keep.tile([P, T], I32, name="table", align_bytes=64)
         table_scales = keep.tile([P, T], U8, name="table_scales", align_bytes=64)
         w_scales = keep.tile([P, 3 * N], U8, name="w_scales", align_bytes=64)
+        w4 = [keep.tile([P, 2 * N], U8, name=name, align_bytes=64) for name in ("wa", "wb", "wc")]
         wgo_rows = keep.tile([P, P], F32, name="wgo_rows")
-        pages = [keep.tile([P, T], F32, name="page%d" % i) for i in range(2)]
+        ident = keep.tile([P, P], F32, name="ident")
+        pages = [keep.tile([P, T], F32, name="page%d" % i) for i in range(3)]
+
+        def zero_on_vector(ap, width, zero):
+            nc.vector.memset(ap[:, 0 : width // 2 + 1], zero)
+            nc.vector.memset(ap[:, width // 2 + 1 : width], zero)
 
         nc.gpsimd.memset(table_scales[:].bitcast(I32), 0)
+        zero_on_vector(w_scales[:].bitcast(I32), 3 * N // 4, 0)
         nc.gpsimd.memset(wgo_rows[:], 0.0)
-        nc.gpsimd.dma_start(wgo_rows[0 : J // P, :], wgo[0].rearrange("(b j) -> b j", j=P))
-        ident = keep.tile([P, P], F32, name="ident")
         make_identity(nc, ident[:])
-        nc.vector.memset(w_scales[:].bitcast(I32), 0)
-        nc.vector.memset(pages[0][:], 0.0)
+        zero_on_vector(pages[0], 3 * T // 4, 0.0)
+        nc.gpsimd.memset(pages[0][:, 3 * T // 4 : T], 0.0)
         nc.gpsimd.memset(pages[1][:], 0.0)
+        nc.gpsimd.memset(pages[2][:], 0.0)
         warm = keep.tile([P, 1], F32, name="warm")
         nc.scalar.activation(warm[32:64, :], wgo_rows[32:64, 0:1], ACT.Sigmoid)
 
@@ -59,6 +73,7 @@ def tile_list_rgg_own_kernel(
                 table_scales[32 * q : 32 * q + 4, :].bitcast(I32), tab_scales[0, 4 * q : 4 * q + 4, :].bitcast(I32)
             )
         nc.sync.dma_start(src_list[:], offs)
+        nc.sync.dma_start(wgo_rows[0 : J // P, :], wgo[0].rearrange("(b j) -> b j", j=P))
         nc.sync.dma_start(table[:], tab_words[0].rearrange("p t i -> p (t i)").bitcast(I32))
         for i, scales in enumerate((wa_scales, wb_scales, wc_scales)):
             nc.sync.dma_start(w_scales[0:16, i * N : (i + 1) * N].bitcast(I32), scales[0].bitcast(I32))
@@ -66,37 +81,44 @@ def tile_list_rgg_own_kernel(
             nc.scalar.dma_start(
                 w_scales[32 * q : 32 * q + 4, :].bitcast(I32), w_scales[4 * q : 4 * q + 4, :].bitcast(I32)
             )
-        w4 = [keep.tile([P, 2 * N], U8, name=name, align_bytes=64) for name in ("wa", "wb", "wc")]
         wo_rows = wo.rearrange("(p i) n -> p i n", i=PACK)
+        raw = []
+
+        def load_wo(s):
+            raw.append(reuse.tile([P, PACK, HALF_N], F32, name="wo_raw%d" % s, align_bytes=64, offset=RAW_AT[s]))
+            nc.sync.dma_start(raw[s][:], wo_rows[:, :, s * HALF_N : (s + 1) * HALF_N])
+
         nc.sync.dma_start(w4[0][:].bitcast(I32), wa_words[0].bitcast(I32))
         nc.sync.dma_start(w4[1][:].bitcast(I32), wb_words[0].bitcast(I32))
         nc.sync.dma_start(w4[2][:].bitcast(I32), wc_words[0].bitcast(I32))
+        load_wo(0)
 
         lists = {"dst": dst_list, "src": src_list}
         words = {}
         scales = {}
 
         def gather(store, window, dtype, side, lo, hi, at):
-            got = reuse.tile([P, hi - lo], dtype, name="%s_%d" % (side, at), align_bytes=64, offset=at)
+            name = "%s_%d_%d" % (side, lo, window.shape[1] + (dtype == U8))
+            if at is None:
+                got = keep.tile([P, hi - lo], dtype, name=name, align_bytes=64)
+            else:
+                got = reuse.tile([P, hi - lo], dtype, name=name, align_bytes=64, offset=at)
             nc.vector.tensor_copy(got[:], window.indirect(lists[side][:, lo // 16 : hi // 16]))
             for b in range(lo // P, hi // P):
                 store[side, b] = got[:, b * P - lo : (b + 1) * P - lo]
 
-        def gather_words(side, lo, hi, at):
+        def gather_words(side, lo, hi, at=None):
             gather(words, table[:].bitcast(U32), U32, side, lo, hi, at)
 
-        def gather_scales(side, lo, hi, at):
+        def gather_scales(side, lo, hi, at=None):
             gather(scales, table_scales[:], U8, side, lo, hi, at)
 
         wo_codes = []
         wo_scales = []
 
-        def quantise_wo(s, at):
-            raw = reuse.tile([P, PACK, HALF_N], F32, name="wo_raw%d" % s, align_bytes=64, offset=(23552, 26176)[s])
-            nc.sync.dma_start(raw[:], wo_rows[:, :, s * HALF_N : (s + 1) * HALF_N])
-            grouped = reuse.tile([P, HALF_N, PACK], BF16, name="grouped%d" % s, align_bytes=64, offset=at)
+        def quantise_wo(s, grouped):
             nc.scalar.copy(
-                grouped[:].rearrange("p (c u) i -> p c i u", u=4), raw[:].rearrange("p i (c u) -> p c i u", u=4)
+                grouped[:].rearrange("p (c u) i -> p c i u", u=4), raw[s][:].rearrange("p i (c u) -> p c i u", u=4)
             )
             codes = keep.tile([P, HALF_N], U32, name="wo_codes%d" % s, align_bytes=64)
             plane = keep.tile([P, HALF_N], U8, name="wo_scales%d" % s, align_bytes=64)
@@ -166,17 +188,18 @@ def tile_list_rgg_own_kernel(
         wgo_col = keep.tile([P, J // P], F32, name="wgo_col")
         nc.scalar.copy(wgo_col[:], wgo_bank[:, 0 : J // P])
 
-        gather_scales("dst", 0, HALF_J, 6144)
-        gather_scales("src", 0, HALF_J, 6656)
-        gather_words("dst", 0, 256, 7168)
-        gather_words("src", 0, 256, 8192)
-        gather_words("dst", 256, 512, 9216)
-        gather_words("src", 256, 512, 10240)
-        gather_scales("dst", HALF_J, J, 0)
-        quantise_wo(0, 2048)
-        gather_scales("src", HALF_J, J, 23616)
-        gather_words("dst", HALF_J, J, 21568)
-        gather_words("src", HALF_J, J, 24128)
+        gather_scales("dst", 0, HALF_J)
+        gather_scales("src", 0, HALF_J)
+        gather_words("dst", 0, QUARTER_J)
+        gather_words("src", 0, QUARTER_J)
+        gather_words("dst", QUARTER_J, HALF_J)
+        gather_words("src", QUARTER_J, HALF_J)
+        gather_scales("dst", HALF_J, J)
+        quantise_wo(0, keep.tile([P, HALF_N, PACK], BF16, name="rounded0", align_bytes=64))
+        gather_scales("src", HALF_J, J, LATE_SRC_SCALES_AT)
+        gather_words("dst", HALF_J, J, LATE_DST_WORDS_AT)
+        gather_words("src", HALF_J, J, LATE_SRC_WORDS_AT)
+        load_wo(1)
         unit([(0, 0, 2)])
         scatter(0, 0, 2)
         unit([(1, 0, 2)])
@@ -184,13 +207,11 @@ def tile_list_rgg_own_kernel(
         unit([(0, 2, 4), (1, 2, 4)])
         scatter(0, 2, 4)
         scatter(1, 2, 4)
-        unit([(0, 4, 8)], reuse.tile([P, 4, P], F32, name="eta_early", align_bytes=64, offset=12288))
+        unit([(0, 4, 8)], reuse.tile([P, 4, P], F32, name="fourth_gate", align_bytes=64, offset=FOURTH_GATE_AT))
         scatter(0, 4, 8)
-        pages.append(reuse.tile([P, T], F32, name="page2", align_bytes=64, offset=13312))
-        nc.gpsimd.memset(pages[2][:], 0.0)
         unit([(1, 4, 8)])
         scatter(1, 4, 8)
-        quantise_wo(1, 11264)
+        quantise_wo(1, reuse.tile([P, HALF_N, PACK], BF16, name="rounded1", align_bytes=64, offset=SECOND_ROUNDED_AT))
         for b_lo in (0, 4):
             for r in (2, 3):
                 unit([(r, b_lo, b_lo + 4)])

@@ -68,12 +68,12 @@ def tile_list_rgg_own_kernel(
         nc.scalar.activation(warm[32:64, :], wgo_rows[32:64, 0:1], ACT.Sigmoid)
 
         nc.sync.dma_start(dst_list[:], offs2)
+        nc.sync.dma_start(w4[0][:].bitcast(I32), wa_words[0].bitcast(I32))
         for q, queue in ((2, nc.scalar), (0, nc.sync), (3, nc.sync), (1, nc.sync)):
             queue.dma_start(
                 table_scales[32 * q : 32 * q + 4, :].bitcast(I32), tab_scales[0, 4 * q : 4 * q + 4, :].bitcast(I32)
             )
         nc.sync.dma_start(src_list[:], offs)
-        nc.sync.dma_start(wgo_rows[0 : J // P, :], wgo[0].rearrange("(b j) -> b j", j=P))
         nc.sync.dma_start(table[:], tab_words[0].rearrange("p t i -> p (t i)").bitcast(I32))
         for i, scales in enumerate((wa_scales, wb_scales, wc_scales)):
             nc.sync.dma_start(w_scales[0:16, i * N : (i + 1) * N].bitcast(I32), scales[0].bitcast(I32))
@@ -88,10 +88,10 @@ def tile_list_rgg_own_kernel(
             raw.append(reuse.tile([P, PACK, HALF_N], F32, name="wo_raw%d" % s, align_bytes=64, offset=RAW_AT[s]))
             nc.sync.dma_start(raw[s][:], wo_rows[:, :, s * HALF_N : (s + 1) * HALF_N])
 
-        nc.sync.dma_start(w4[0][:].bitcast(I32), wa_words[0].bitcast(I32))
+        nc.sync.dma_start(wgo_rows[0 : J // P, :], wgo[0].rearrange("(b j) -> b j", j=P))
         nc.sync.dma_start(w4[1][:].bitcast(I32), wb_words[0].bitcast(I32))
-        nc.sync.dma_start(w4[2][:].bitcast(I32), wc_words[0].bitcast(I32))
         load_wo(0)
+        nc.sync.dma_start(w4[2][:].bitcast(I32), wc_words[0].bitcast(I32))
 
         lists = {"dst": dst_list, "src": src_list}
         words = {}
@@ -142,23 +142,23 @@ def tile_list_rgg_own_kernel(
         def unit(runs, eta=None):
             tiles = [(r, b) for r, b_lo, b_hi in runs for b in range(b_lo, b_hi)]
             n = len(tiles)
-            za = psum.tile([P, 4, P], F32, name="za")
-            ms = psum.tile([P, 4, P], F32, name="ms")
-            ow = psum.tile([P, 4, P], F32, name="ow")
+            za = psum.tile([P, 4, P], F32, name="za", bufs=3)
+            ms = psum.tile([P, 4, P], F32, name="ms", bufs=3)
             for i, (r, b) in enumerate(tiles):
                 mx(za[:, i, :], "dst", b, *fp4(0, r), True, False)
                 mx(za[:, i, :], "src", b, *fp4(1, r), False, True)
             for i, (r, b) in enumerate(tiles):
                 mx(ms[:, i, :], "src", b, *fp4(2, r), True, True)
-            for i, (r, b) in enumerate(tiles):
-                s, lo = divmod(r * P, HALF_N)
-                mx(ow[:, i, :], "dst", b, wo_codes[s][:, lo : lo + P].bitcast(FP8X4), wo_scales[s][:, lo : lo + P], True, True)
             if eta is None:
                 eta = work.tile([P, 4, P], F32, name="eta")
             message = work.tile([P, 4, P], F32, name="message")
             own = work.tile([P, 4, P], F32, name="own")
             gated = work.tile([P, 4, P], F32, name="gated")
             nc.scalar.activation(eta[:, 0:n, :], za[:, 0:n, :], ACT.Sigmoid)
+            ow = za
+            for i, (r, b) in enumerate(tiles):
+                s, lo = divmod(r * P, HALF_N)
+                mx(ow[:, i, :], "dst", b, wo_codes[s][:, lo : lo + P].bitcast(FP8X4), wo_scales[s][:, lo : lo + P], True, True)
             for i, (r, b) in enumerate(tiles):
                 nc.scalar.activation(message[:, i, :], ms[:, i, :], ACT.Copy, scale=wgo_col[:, b : b + 1])
             nc.gpsimd.tensor_tensor(gated[:, 0:n, :], eta[:, 0:n, :], message[:, 0:n, :], MULT)

@@ -69,10 +69,8 @@ def tile_list_rgg_own_kernel(
 
         nc.sync.dma_start(dst_list[:], offs2)
         nc.sync.dma_start(w4[0][:].bitcast(I32), wa_words[0].bitcast(I32))
-        for q, queue in ((2, nc.scalar), (0, nc.sync), (3, nc.sync), (1, nc.sync)):
-            queue.dma_start(
-                table_scales[32 * q : 32 * q + 4, :].bitcast(I32), tab_scales[0, 4 * q : 4 * q + 4, :].bitcast(I32)
-            )
+        for r, queue in enumerate((nc.scalar, nc.sync, nc.sync, nc.sync)):
+            queue.dma_start(table_scales[r:P:32, :].bitcast(I32), tab_scales[0, r:16:4, :].bitcast(I32))
         nc.sync.dma_start(src_list[:], offs)
         nc.sync.dma_start(table[:], tab_words[0].rearrange("p t i -> p (t i)").bitcast(I32))
         for i, scales in enumerate((wa_scales, wb_scales, wc_scales)):
@@ -188,13 +186,12 @@ def tile_list_rgg_own_kernel(
         wgo_col = keep.tile([P, J // P], F32, name="wgo_col")
         nc.scalar.copy(wgo_col[:], wgo_bank[:, 0 : J // P])
 
-        gather_scales("dst", 0, HALF_J)
+        gather_scales("dst", 0, J)
         gather_scales("src", 0, HALF_J)
         gather_words("dst", 0, QUARTER_J)
         gather_words("src", 0, QUARTER_J)
         gather_words("dst", QUARTER_J, HALF_J)
         gather_words("src", QUARTER_J, HALF_J)
-        gather_scales("dst", HALF_J, J)
         quantise_wo(0, keep.tile([P, HALF_N, PACK], BF16, name="rounded0", align_bytes=64))
         gather_scales("src", HALF_J, J, LATE_SRC_SCALES_AT)
         gather_words("dst", HALF_J, J, LATE_DST_WORDS_AT)

from contextlib import ExitStack

import concourse.mybir as mybir
from concourse.masks import make_identity

K, N, T, J = 512, 512, 2048, 1024
FLOPS = 2 * 4 * K * N * J

F32 = mybir.dt.float32
BF16 = mybir.dt.bfloat16
I32 = mybir.dt.int32
U32 = mybir.dt.uint32
U16 = mybir.dt.uint16
U8 = mybir.dt.uint8
FP8X4 = mybir.dt.float8_e4m3fn_x4
FP4X4 = mybir.dt.float4_e2m1fn_x4
ACT = mybir.ActivationFunctionType
MULT = mybir.AluOpType.mult

P = 128
PACK = 4
QUARTER_J = J // 4
HALF_J = J // 2
HALF_N = N // 2
PAGE_OF_ROWS = (0, 1, 2, 0)

RAW_AT = (2048, 5696)
LATE_DST_WORDS_AT = 64
LATE_SRC_SCALES_AT = 3136
LATE_SRC_WORDS_AT = 3648
SECOND_ROUNDED_AT = 9792
FOURTH_GATE_AT = 10816


def tile_list_rgg_own_kernel(
    tc, tab_words, tab_scales, wa_words, wa_scales, wb_words, wb_scales, wc_words, wc_scales, wo, wgo, offs, offs2, out
):
    nc = tc.nc
    with ExitStack() as ctx:
        keep = ctx.enter_context(tc.tile_pool(name="keep", bufs=1))
        reuse = ctx.enter_context(tc.tile_pool(name="reuse", bufs=1))
        work = ctx.enter_context(tc.tile_pool(name="work", bufs=4))
        psum = ctx.enter_context(tc.psum_pool(name="psum", bufs=2))

        src_list = keep.tile([P, J // 16], U16, name="src_list")
        dst_list = keep.tile([P, J // 16], U16, name="dst_list")
        table = keep.tile([P, T], I32, name="table", align_bytes=64)
        table_scales = keep.tile([P, T], U8, name="table_scales", align_bytes=64)
        w_scales = keep.tile([P, 3 * N], U8, name="w_scales", align_bytes=64)
        w4 = [keep.tile([P, 2 * N], U8, name=name, align_bytes=64) for name in ("wa", "wb", "wc")]
        wgo_rows = keep.tile([P, P], F32, name="wgo_rows")
        ident = keep.tile([P, P], F32, name="ident")
        pages = [keep.tile([P, T], F32, name="page%d" % i) for i in range(3)]

        def zero_on_vector(ap, width, zero):
            nc.vector.memset(ap[:, 0 : width // 2 + 1], zero)
            nc.vector.memset(ap[:, width // 2 + 1 : width], zero)

        nc.gpsimd.memset(table_scales[:].bitcast(I32), 0)
        zero_on_vector(w_scales[:].bitcast(I32), 3 * N // 4, 0)
        nc.gpsimd.memset(wgo_rows[:], 0.0)
        make_identity(nc, ident[:])
        zero_on_vector(pages[0], 3 * T // 4, 0.0)
        nc.gpsimd.memset(pages[0][:, 3 * T // 4 : T], 0.0)
        nc.gpsimd.memset(pages[1][:], 0.0)
        nc.gpsimd.memset(pages[2][:], 0.0)
        warm = keep.tile([P, 1], F32, name="warm")
        nc.scalar.activation(warm[32:64, :], wgo_rows[32:64, 0:1], ACT.Sigmoid)

        nc.sync.dma_start(dst_list[:], offs2)
        nc.sync.dma_start(w4[0][:].bitcast(I32), wa_words[0].bitcast(I32))
        for r, queue in enumerate((nc.scalar, nc.sync, nc.sync, nc.sync)):
            queue.dma_start(table_scales[r:P:32, :].bitcast(I32), tab_scales[0, r:16:4, :].bitcast(I32))
        nc.sync.dma_start(src_list[:], offs)
        nc.sync.dma_start(table[:], tab_words[0].rearrange("p t i -> p (t i)").bitcast(I32))
        for i, scales in enumerate((wa_scales, wb_scales, wc_scales)):
            nc.sync.dma_start(w_scales[0:16, i * N : (i + 1) * N].bitcast(I32), scales[0].bitcast(I32))
        for q in range(1, 4):
            nc.scalar.dma_start(
                w_scales[32 * q : 32 * q + 4, :].bitcast(I32), w_scales[4 * q : 4 * q + 4, :].bitcast(I32)
            )
        wo_rows = wo.rearrange("(p i) n -> p i n", i=PACK)
        raw = []

        def load_wo(s):
            raw.append(reuse.tile([P, PACK, HALF_N], F32, name="wo_raw%d" % s, align_bytes=64, offset=RAW_AT[s]))
            nc.sync.dma_start(raw[s][:], wo_rows[:, :, s * HALF_N : (s + 1) * HALF_N])

        nc.sync.dma_start(wgo_rows[0 : J // P, :], wgo[0].rearrange("(b j) -> b j", j=P))
        nc.sync.dma_start(w4[1][:].bitcast(I32), wb_words[0].bitcast(I32))
        load_wo(0)
        nc.sync.dma_start(w4[2][:].bitcast(I32), wc_words[0].bitcast(I32))

        lists = {"dst": dst_list, "src": src_list}
        words = {}
        scales = {}

        def gather(store, window, dtype, side, lo, hi, at):
            name = "%s_%d_%d" % (side, lo, window.shape[1] + (dtype == U8))
            if at is None:
                got = keep.tile([P, hi - lo], dtype, name=name, align_bytes=64)
            else:
                got = reuse.tile([P, hi - lo], dtype, name=name, align_bytes=64, offset=at)
            nc.vector.tensor_copy(got[:], window.indirect(lists[side][:, lo // 16 : hi // 16]))
            for b in range(lo // P, hi // P):
                store[side, b] = got[:, b * P - lo : (b + 1) * P - lo]

        def gather_words(side, lo, hi, at=None):
            gather(words, table[:].bitcast(U32), U32, side, lo, hi, at)

        def gather_scales(side, lo, hi, at=None):
            gather(scales, table_scales[:], U8, side, lo, hi, at)

        wo_codes = []
        wo_scales = []

        def quantise_wo(s, grouped):
            nc.scalar.copy(
                grouped[:].rearrange("p (c u) i -> p c i u", u=4), raw[s][:].rearrange("p i (c u) -> p c i u", u=4)
            )
            codes = keep.tile([P, HALF_N], U32, name="wo_codes%d" % s, align_bytes=64)
            plane = keep.tile([P, HALF_N], U8, name="wo_scales%d" % s, align_bytes=64)
            nc.vector.quantize_mx(
                out=codes[:].bitcast(FP8X4), scales=plane[:], in_=grouped[:].rearrange("p n i -> p (n i)")
            )
            wo_codes.append(codes)
            wo_scales.append(plane)

        def mx(bank, side, b, rhs, rhs_scale, start, stop):
            nc.tensor.matmul_mx(
                out=bank, lhsT=words[side, b].bitcast(FP8X4), lhsT_scale=scales[side, b],
                rhs=rhs, rhs_scale=rhs_scale, start=start, stop=stop,
            )

        def fp4(i, r):
            return w4[i][:, 2 * r * P : 2 * (r + 1) * P].bitcast(FP4X4), w_scales[:, i * N + r * P : i * N + (r + 1) * P]

        stage = [keep.tile([P, J], F32, name="stage%d" % r) for r in range(N // P)]

        def unit(runs, eta=None):
            tiles = [(r, b) for r, b_lo, b_hi in runs for b in range(b_lo, b_hi)]
            n = len(tiles)
            za = psum.tile([P, 4, P], F32, name="za", bufs=3)
            ms = psum.tile([P, 4, P], F32, name="ms", bufs=3)
            for i, (r, b) in enumerate(tiles):
                mx(za[:, i, :], "dst", b, *fp4(0, r), True, False)
                mx(za[:, i, :], "src", b, *fp4(1, r), False, True)
            for i, (r, b) in enumerate(tiles):
                mx(ms[:, i, :], "src", b, *fp4(2, r), True, True)
            if eta is None:
                eta = work.tile([P, 4, P], F32, name="eta")
            message = work.tile([P, 4, P], F32, name="message")
            own = work.tile([P, 4, P], F32, name="own")
            gated = work.tile([P, 4, P], F32, name="gated")
            nc.scalar.activation(eta[:, 0:n, :], za[:, 0:n, :], ACT.Sigmoid)
            ow = za
            for i, (r, b) in enumerate(tiles):
                s, lo = divmod(r * P, HALF_N)
                mx(ow[:, i, :], "dst", b, wo_codes[s][:, lo : lo + P].bitcast(FP8X4), wo_scales[s][:, lo : lo + P], True, True)
            for i, (r, b) in enumerate(tiles):
                nc.scalar.activation(message[:, i, :], ms[:, i, :], ACT.Copy, scale=wgo_col[:, b : b + 1])
            nc.gpsimd.tensor_tensor(gated[:, 0:n, :], eta[:, 0:n, :], message[:, 0:n, :], MULT)
            for i, (r, b) in enumerate(tiles):
                nc.scalar.activation(own[:, i, :], ow[:, i, :], ACT.Copy, scale=wgo_col[:, b : b + 1])
            bank = psum.tile([P, 4 * P], F32, name="turned", tag="turned")
            for i in range(n):
                cols = slice(i * P, (i + 1) * P)
                nc.tensor.matmul(bank[:, cols], own[:, i, :], ident[:], start=True, stop=False, is_transpose=True)
                nc.tensor.matmul(bank[:, cols], gated[:, i, :], ident[:], start=False, stop=True, is_transpose=True)
            at = 0
            for r, b_lo, b_hi in runs:
                width = (b_hi - b_lo) * P
                nc.scalar.copy(stage[r][:, b_lo * P : b_hi * P], bank[:, at : at + width])
                at = at + width

        def scatter(r, b_lo, b_hi):
            page = pages[PAGE_OF_ROWS[r]]
            nc.vector.tensor_copy(
                page[:].indirect(dst_list[:, b_lo * P // 16 : b_hi * P // 16]), stage[r][:, b_lo * P : b_hi * P]
            )
            if b_hi == J // P:
                nc.sync.dma_start(out[r * P : (r + 1) * P, :], page[:])

        wgo_bank = psum.tile([P, 4 * P], F32, name="wgo_bank", tag="turned")
        nc.tensor.transpose(wgo_bank[:, 0:P], wgo_rows[:], ident[:])
        wgo_col = keep.tile([P, J // P], F32, name="wgo_col")
        nc.scalar.copy(wgo_col[:], wgo_bank[:, 0 : J // P])

        gather_scales("dst", 0, J)
        gather_scales("src", 0, HALF_J)
        gather_words("dst", 0, QUARTER_J)
        gather_words("src", 0, QUARTER_J)
        gather_words("dst", QUARTER_J, HALF_J)
        gather_words("src", QUARTER_J, HALF_J)
        quantise_wo(0, keep.tile([P, HALF_N, PACK], BF16, name="rounded0", align_bytes=64))
        gather_scales("src", HALF_J, J, LATE_SRC_SCALES_AT)
        gather_words("dst", HALF_J, J, LATE_DST_WORDS_AT)
        gather_words("src", HALF_J, J, LATE_SRC_WORDS_AT)
        load_wo(1)
        unit([(0, 0, 2)])
        scatter(0, 0, 2)
        unit([(1, 0, 2)])
        scatter(1, 0, 2)
        unit([(0, 2, 4), (1, 2, 4)])
        scatter(0, 2, 4)
        scatter(1, 2, 4)
        unit([(0, 4, 8)], reuse.tile([P, 4, P], F32, name="fourth_gate", align_bytes=64, offset=FOURTH_GATE_AT))
        scatter(0, 4, 8)
        unit([(1, 4, 8)])
        scatter(1, 4, 8)
        quantise_wo(1, reuse.tile([P, HALF_N, PACK], BF16, name="rounded1", align_bytes=64, offset=SECOND_ROUNDED_AT))
        for b_lo in (0, 4):
            for r in (2, 3):
                unit([(r, b_lo, b_lo + 4)])
                scatter(r, b_lo, b_lo + 4)
